import numpy as np
import ml_dtypes


def mxq(x, axis, fmt="e4m3"):
    dtype, down = {"e4m3": (ml_dtypes.float8_e4m3fn, 7), "e5m2": (ml_dtypes.float8_e5m2, 14)}[fmt]
    v = np.moveaxis(np.asarray(x, np.float32).astype(ml_dtypes.bfloat16).astype(np.float64), axis, -1)
    blocks = v.reshape(v.shape[:-1] + (-1, 32))
    amax = np.abs(blocks).max(-1, keepdims=True)
    byte = np.maximum(np.where(amax > 0, np.frexp(amax)[1] - 1 + 127, 0) - down, 1)
    scale = np.exp2(byte - 127.0)
    codes = (blocks / scale).astype(np.float32).astype(dtype).astype(np.float64)
    return np.moveaxis((codes * scale).reshape(v.shape), -1, axis)


WIDE = False


def mx_kscale(k):
    if not WIDE:
        return np.ones(k)
    levels = np.array([10, -10, 5, -5, 0])
    if k % 512:
        return np.exp2(np.random.permutation(np.resize(levels, k // 32))).repeat(32)
    a = np.empty((k // 512, 16))
    for p in range(k // 512):
        a[p, :8] = np.random.permutation(np.resize(levels, 8))
        for g in range(8):
            far = levels[np.abs(levels - a[p, g]) >= 10]
            a[p, g + 8] = far[np.random.randint(len(far))]
    return np.exp2(a.ravel()).repeat(32)


def f64(x):
    return np.asarray(x).astype(np.float64)


def striped(idx):
    return np.tile(np.asarray(idx).reshape(-1, 16).T, (8, 1)).astype(np.uint16)


def unstriped(offs):
    return offs[:16].T.reshape(-1).astype(np.int64)


E2M1 = np.array([0.0, 0.5, 1.0, 1.5, 2.0, 3.0, 4.0, 6.0, -0.0, -0.5, -1.0, -1.5, -2.0, -3.0, -4.0, -6.0])


def pack_weight(w, fmt):
    k, n = w.shape
    w = f64(np.asarray(w, np.float32).astype(ml_dtypes.bfloat16)).reshape(k // 32, 32, n)
    amax = np.abs(w).max(1)
    if fmt == "e4m3":
        byte = np.frexp(amax)[1] - 1 + 127 - 7
    else:
        mant, ex = np.frexp(amax / 6.0)
        byte = np.where(mant > 0.5, ex, ex - 1) + 127
    byte = np.clip(np.where(amax > 0, byte, 1), 1, 254)
    scaled = (w * np.exp2(127.0 - byte)[:, None, :]).reshape(k, n).astype(np.float32)
    by_word = np.ascontiguousarray(scaled.reshape(k // 512, 128, 4, n).transpose(0, 1, 3, 2))
    if fmt == "e4m3":
        words = by_word.astype(ml_dtypes.float8_e4m3fn).view(np.uint8)
    else:
        c = by_word.astype(ml_dtypes.float4_e2m1fn).view(np.uint8) & 0xF
        words = (c[..., 0::2] | (c[..., 1::2] << 4)).reshape(k // 512, 128, 2 * n)
    return np.ascontiguousarray(words), np.ascontiguousarray(byte.astype(np.uint8).reshape(k // 512, 16, n))


def unpack_weight(words, scales, fmt):
    g, _, n = scales.shape
    words = np.ascontiguousarray(words).reshape(g, 128, n, -1)
    if fmt == "e4m3":
        vals = words.view(ml_dtypes.float8_e4m3fn).astype(np.float64)
    else:
        nib = np.empty((g, 128, n, 4), np.uint8)
        nib[..., 0::2] = words & 0xF
        nib[..., 1::2] = words >> 4
        vals = E2M1[nib]
    vals = vals * np.repeat(np.exp2(scales.astype(np.float64) - 127.0), 8, axis=1)[..., None]
    return vals.transpose(0, 1, 3, 2).reshape(g * 512, n)


def bf(x):
    return np.asarray(x, np.float32).astype(ml_dtypes.bfloat16)


def planes(Y):
    r, m = Y.shape
    b = f64(bf(Y)).reshape(r // 32, 32, m)
    amax = np.abs(b).max(1)
    byte = np.clip(np.where(amax > 0, np.frexp(amax)[1] - 1 + 127 - 7, 1), 1, 254)
    codes = (b * np.exp2(127.0 - byte)[:, None, :]).reshape(r, m).astype(np.float32).astype(ml_dtypes.float8_e4m3fn).view(np.uint8)
    words = codes.reshape(r // 512, 128, 4, m).transpose(0, 1, 3, 2)
    return np.ascontiguousarray(words), np.ascontiguousarray(byte.astype(np.uint8).reshape(r // 512, 16, m))


D, T, I, J, U, G, Q = 512, 1024, 512, 512, 2048, 512, 512


def setup_inputs():
    n = np.random.standard_normal
    idx = np.random.permutation(T)[:I]
    idx2 = np.random.permutation(T)[:J]
    idx3 = np.random.permutation(U)[:G]
    fd = mx_kscale(D)
    candp = pack_weight(n((D, U)) / fd[:, None], "e2m1")
    return {
        "query": (n((D, Q)) * 1.0 / np.sqrt(D) * fd[:, None]).astype(np.float32),
        "rel": (n((D, T)) * 0.5 * fd[:, None]).astype(np.float32),
        "irr": (n((D, T)) * 0.5 * fd[:, None]).astype(np.float32),
        "fa": (np.random.uniform(0.5, 1.0, (D, 1))).astype(np.float32),
        "fb": (np.random.uniform(0.2, 0.7, (D, 1))).astype(np.float32),
        "cand_words": candp[0],
        "cand_scales": candp[1],
        "offs": striped(idx),
        "offs2": striped(idx2),
        "offs3": striped(idx3),
    }


def reference(query, rel, irr, fa, fb, cand_words, cand_scales, offs, offs2, offs3):
    idx = unstriped(offs)
    idx2 = unstriped(offs2)
    idx3 = unstriped(offs3)
    candu = unpack_weight(cand_words, cand_scales, "e2m1")
    m = f64(fa) * np.mean(f64(rel)[:, idx], axis=1, keepdims=True) - f64(fb) * np.mean(f64(irr)[:, idx2], axis=1, keepdims=True)
    x = f64(query) + m
    xq = mxq(x, 0, "e4m3")
    candidx3g = candu[:, idx3]
    y = xq.T @ candidx3g
    words, scales = planes(y)
    return y, words, scales

@@ -1,0 +1,147 @@
+from contextlib import ExitStack
+
+import concourse.mybir as mybir
+
+D, T, U, Q, G = 512, 1024, 2048, 512, 512
+SLOTS = 512
+P = 128
+PACK = 4
+CHUNK = 128
+CHUNKS = G // CHUNK
+HALF = G // 2
+
+FLOPS = 2 * D * Q * G
+
+F32 = mybir.dt.float32
+BF16 = mybir.dt.bfloat16
+I32 = mybir.dt.int32
+U32 = mybir.dt.uint32
+U16 = mybir.dt.uint16
+U8 = mybir.dt.uint8
+FP8X4 = mybir.dt.float8_e4m3fn_x4
+FP4X4 = mybir.dt.float4_e2m1fn_x4
+IDENT = mybir.ActivationFunctionType.Identity
+ADD = mybir.AluOpType.add
+
+
+def tile_attend_rocchio_pl_kernel(tc, query, rel, irr, fa, fb, cand_words, cand_scales, offs, offs2, offs3,
+                                   out_0, out_1, out_2):
+    nc = tc.nc
+    with ExitStack() as ctx:
+        held = ctx.enter_context(tc.tile_pool(name="held", bufs=1))
+        psum = ctx.enter_context(tc.psum_pool(name="psum", bufs=1))
+
+        rel_list = held.tile([P, SLOTS // 16], U16, name="rel_list")
+        irr_list = held.tile([P, SLOTS // 16], U16, name="irr_list")
+        cand_list = held.tile([P, G // 16], U16, name="cand_list")
+        rel_rows = [held.tile([P, T], F32, name="rel_rows%d" % t) for t in range(PACK)]
+        irr_rows = [held.tile([P, T], F32, name="irr_rows%d" % t) for t in range(PACK)]
+        query_rows = [held.tile([P, Q], F32, name="query_rows%d" % t) for t in range(PACK)]
+        words_all = held.tile([P, U], U16, name="words_all")
+        scales_all = held.tile([P, U], U8, name="scales_all")
+        fa_sb = held.tile([P, PACK], F32, name="fa_sb")
+        fb_sb = held.tile([P, PACK], F32, name="fb_sb")
+        fa_scaled = held.tile([P, PACK], F32, name="fa_scaled")
+        fb_scaled = held.tile([P, PACK], F32, name="fb_scaled")
+
+        rel_v = rel.rearrange("(p t) c -> p t c", t=PACK)
+        irr_v = irr.rearrange("(p t) c -> p t c", t=PACK)
+        query_v = query.rearrange("(p t) c -> p t c", t=PACK)
+        scales_v = cand_scales[0].bitcast(I32)
+
+        nc.vector.memset(scales_all[:].bitcast(I32), 0)
+        nc.gpsimd.dma_start(fa_sb[:], fa.rearrange("(p t) o -> p (t o)", t=PACK))
+        nc.gpsimd.dma_start(fb_sb[:], fb.rearrange("(p t) o -> p (t o)", t=PACK))
+
+        def load_scale_rows(quad):
+            nc.scalar.dma_start(scales_all[32 * quad:32 * quad + 4, :].bitcast(I32), scales_v[4 * quad:4 * quad + 4, :])
+
+        nc.sync.dma_start(cand_list[:], offs3)
+        nc.sync.dma_start(rel_rows[0][:], rel_v[:, 0, :])
+        for quad in range(4):
+            load_scale_rows(quad)
+        nc.sync.dma_start(rel_list[:], offs)
+        nc.sync.dma_start(irr_rows[0][:], irr_v[:, 0, :])
+        nc.sync.dma_start(irr_list[:], offs2)
+        nc.sync.dma_start(query_rows[0][:], query_v[:, 0, :])
+        for t in range(1, PACK):
+            nc.sync.dma_start(rel_rows[t][:], rel_v[:, t, :])
+            nc.sync.dma_start(irr_rows[t][:], irr_v[:, t, :])
+            if t == 1:
+                nc.sync.dma_start(query_rows[1][:], query_v[:, 1, :])
+        nc.sync.dma_start(words_all[:].bitcast(I32), cand_words[0].bitcast(I32))
+        for t in (2, 3):
+            nc.sync.dma_start(query_rows[t][:], query_v[:, t, :])
+
+        nc.scalar.activation(fa_scaled[:], fa_sb[:], IDENT, scale=1.0 / (SLOTS * SLOTS))
+        nc.scalar.activation(fb_scaled[:], fb_sb[:], IDENT, scale=-1.0 / SLOTS)
+
+        cand_scale = held.tile([P, G], U8, name="cand_scale", align_bytes=64)
+        cand_code = [held.tile([P, HALF], U16, name="cand_code%d" % h, align_bytes=64) for h in range(2)]
+        nc.vector.tensor_copy(cand_scale[:], scales_all[:].indirect(cand_list[:]))
+
+        x_bf = held.tile([P, PACK, P, PACK], BF16, name="x_bf", align_bytes=64)
+        x_view = x_bf[:].rearrange("p r s t -> p t s r")
+        shift = []
+
+        def query_view(t):
+            return query_rows[t][:].rearrange("p (s r) -> p s r", r=PACK)
+
+        for t in range(PACK):
+            rel_pick = held.tile([P, SLOTS], F32, name="rel_pick%d" % t)
+            irr_pick = held.tile([P, SLOTS], F32, name="irr_pick%d" % t)
+            rel_terms = held.tile([P, SLOTS], F32, name="rel_terms%d" % t)
+            irr_terms = held.tile([P, SLOTS], F32, name="irr_terms%d" % t)
+            rel_share = held.tile([P, 1], F32, name="rel_share%d" % t)
+            shift_t = held.tile([P, 1], F32, name="shift%d" % t)
+            shift.append(shift_t)
+            nc.vector.tensor_copy(rel_pick[:], rel_rows[t][:].indirect(rel_list[:]))
+            nc.scalar.activation(rel_terms[:], rel_pick[:], IDENT, scale=fa_scaled[:, t:t + 1], accum_out=rel_share[:])
+            nc.vector.tensor_copy(irr_pick[:], irr_rows[t][:].indirect(irr_list[:]))
+            nc.scalar.activation(irr_terms[:], irr_pick[:], IDENT, scale=fb_scaled[:, t:t + 1], bias=rel_share[:],
+                                 accum_out=shift_t[:])
+            if t < 2:
+                nc.scalar.activation(x_view[:, t], query_view(t), IDENT, bias=shift_t[:])
+
+        nc.vector.tensor_copy(cand_code[0][:], words_all[:].indirect(cand_list[:, 0:HALF // 16]))
+        for t in (2, 3):
+            nc.vector.tensor_scalar(x_view[:, t, :, 0:3], query_view(t)[:, :, 0:3], shift[t][:], None, ADD)
+            nc.scalar.activation(x_view[:, t, :, 3], query_view(t)[:, :, 3], IDENT, bias=shift[t][:])
+
+        x_code = held.tile([P, Q], U32, name="x_code", align_bytes=64)
+        x_scale = held.tile([P, Q], U8, name="x_scale", align_bytes=64)
+        for r in range(PACK):
+            cols = slice(r * P, (r + 1) * P)
+            nc.vector.quantize_mx(out=x_code[:, cols].bitcast(FP8X4), scales=x_scale[:, cols],
+                                  in_=x_bf[:, r].rearrange("p s t -> p (s t)"))
+        nc.vector.tensor_copy(cand_code[1][:], words_all[:].indirect(cand_list[:, HALF // 16:G // 16]))
+
+        y_code = held.tile([P, G], U32, name="y_code", align_bytes=64)
+        y_scale = held.tile([P, G], U8, name="y_scale", align_bytes=64)
+        out0_v = out_0.rearrange("(p r) g -> p r g", r=PACK)
+        out1_v = out_1[0].rearrange("p c t -> p (c t)").bitcast(I32)
+        out2_v = out_2[0].bitcast(I32)
+        y_half = [held.tile([P, PACK, HALF], F32, name="y_half%d" % h) for h in range(2)]
+        for c in range(CHUNKS):
+            h, local = divmod(c * CHUNK, HALF)
+            cols = slice(c * CHUNK, (c + 1) * CHUNK)
+            bank = psum.tile([P, PACK, CHUNK], F32, name="bank%d" % c)
+            for r in range(PACK):
+                rows = slice(r * P, (r + 1) * P)
+                nc.tensor.matmul_mx(out=bank[:, r, :], lhsT=x_code[:, rows].bitcast(FP8X4), lhsT_scale=x_scale[:, rows],
+                                    rhs=cand_code[h][:, local:local + CHUNK].bitcast(FP4X4), rhs_scale=cand_scale[:, cols],
+                                    start=True, stop=True)
+            y_chunk = y_half[h][:, :, local:local + CHUNK]
+            nc.scalar.copy(y_chunk, bank[:])
+            y_bf = held.tile([P, CHUNK, PACK], BF16, name="y_bf%d" % c, align_bytes=64)
+            nc.vector.tensor_copy(y_bf[:].rearrange("p (c i) r -> p c r i", i=4),
+                                  y_chunk.rearrange("p r (c i) -> p c r i", i=4))
+            nc.vector.quantize_mx(out=y_code[:, cols].bitcast(FP8X4), scales=y_scale[:, cols],
+                                  in_=y_bf[:].rearrange("p g r -> p (g r)"))
+            if local + CHUNK == HALF:
+                half_cols = slice(h * HALF, (h + 1) * HALF)
+                nc.sync.dma_start(out0_v[:, :, half_cols], y_half[h][:])
+                nc.sync.dma_start(out1_v[:, half_cols], y_code[:, half_cols].bitcast(I32))
+        for quad in range(4):
+            queue = nc.sync if quad % 2 == 0 else nc.scalar
+            queue.dma_start(out2_v[4 * quad:4 * quad + 4, :], y_scale[32 * quad:32 * quad + 4, :].bitcast(I32))

@@ -35,8 +35,8 @@ def tile_attend_rocchio_pl_kernel(tc, query, rel, irr, fa, fb, cand_words, cand_
         irr_list = held.tile([P, SLOTS // 16], U16, name="irr_list")
         cand_list = held.tile([P, G // 16], U16, name="cand_list")
         rel_rows = [held.tile([P, T], F32, name="rel_rows%d" % t) for t in range(PACK)]
-        irr_rows = [held.tile([P, T], F32, name="irr_rows%d" % t) for t in range(PACK)]
-        query_rows = [held.tile([P, Q], F32, name="query_rows%d" % t) for t in range(PACK)]
+        irr_rows = [held.tile([P, T], F32, name="irr_rows%d" % t, tag="irr_slot%d" % t, align_bytes=64) for t in range(PACK)]
+        query_rows = [held.tile([P, Q], F32, name="query_rows%d" % t, tag="query_slot%d" % t) for t in range(PACK)]
         words_all = held.tile([P, U], U16, name="words_all")
         scales_all = held.tile([P, U], U8, name="scales_all")
         fa_sb = held.tile([P, PACK], F32, name="fa_sb")
@@ -49,17 +49,14 @@ def tile_attend_rocchio_pl_kernel(tc, query, rel, irr, fa, fb, cand_words, cand_
         query_v = query.rearrange("(p t) c -> p t c", t=PACK)
         scales_v = cand_scales[0].bitcast(I32)
 
-        nc.vector.memset(scales_all[:].bitcast(I32), 0)
-        nc.gpsimd.dma_start(fa_sb[:], fa.rearrange("(p t) o -> p (t o)", t=PACK))
-        nc.gpsimd.dma_start(fb_sb[:], fb.rearrange("(p t) o -> p (t o)", t=PACK))
-
-        def load_scale_rows(quad):
-            nc.scalar.dma_start(scales_all[32 * quad:32 * quad + 4, :].bitcast(I32), scales_v[4 * quad:4 * quad + 4, :])
+        picked_scale = held.tile([P, G], U8, name="picked_scale")
+        nc.vector.memset(scales_all[0:112, :].bitcast(I32), 0)
 
         nc.sync.dma_start(cand_list[:], offs3)
+        nc.scalar.dma_start(scales_all[112:128, :].bitcast(I32), scales_v)
         nc.sync.dma_start(rel_rows[0][:], rel_v[:, 0, :])
-        for quad in range(4):
-            load_scale_rows(quad)
+        nc.scalar.dma_start(fa_sb[:], fa.rearrange("(p t) o -> p (t o)", t=PACK))
+        nc.scalar.dma_start(fb_sb[:], fb.rearrange("(p t) o -> p (t o)", t=PACK))
         nc.sync.dma_start(rel_list[:], offs)
         nc.sync.dma_start(irr_rows[0][:], irr_v[:, 0, :])
         nc.sync.dma_start(irr_list[:], offs2)
@@ -69,44 +66,59 @@ def tile_attend_rocchio_pl_kernel(tc, query, rel, irr, fa, fb, cand_words, cand_
             nc.sync.dma_start(irr_rows[t][:], irr_v[:, t, :])
             if t == 1:
                 nc.sync.dma_start(query_rows[1][:], query_v[:, 1, :])
+        nc.sync.dma_start(query_rows[2][:], query_v[:, 2, :])
         nc.sync.dma_start(words_all[:].bitcast(I32), cand_words[0].bitcast(I32))
-        for t in (2, 3):
-            nc.sync.dma_start(query_rows[t][:], query_v[:, t, :])
+        nc.sync.dma_start(query_rows[3][:], query_v[:, 3, :])
 
         nc.scalar.activation(fa_scaled[:], fa_sb[:], IDENT, scale=1.0 / (SLOTS * SLOTS))
         nc.scalar.activation(fb_scaled[:], fb_sb[:], IDENT, scale=-1.0 / SLOTS)
 
-        cand_scale = held.tile([P, G], U8, name="cand_scale", align_bytes=64)
-        cand_code = [held.tile([P, HALF], U16, name="cand_code%d" % h, align_bytes=64) for h in range(2)]
-        nc.vector.tensor_copy(cand_scale[:], scales_all[:].indirect(cand_list[:]))
+        cand_code = [held.tile([P, HALF], U16, name="cand_code0", align_bytes=64)]
+        nc.vector.tensor_copy(picked_scale[:], scales_all[:].indirect(cand_list[:]))
 
-        x_bf = held.tile([P, PACK, P, PACK], BF16, name="x_bf", align_bytes=64)
+        x_bf = held.tile([P, PACK, P, PACK], BF16, name="x_bf", tag="x_slot", align_bytes=64)
         x_view = x_bf[:].rearrange("p r s t -> p t s r")
         shift = []
 
         def query_view(t):
             return query_rows[t][:].rearrange("p (s r) -> p s r", r=PACK)
 
+        def add_shift_scalar(t, lo, hi):
+            nc.scalar.activation(x_view[:, t, :, lo:hi], query_view(t)[:, :, lo:hi], IDENT, bias=shift[t][:])
+
+        def add_shift_vector(t, lo, hi):
+            nc.vector.tensor_scalar(x_view[:, t, :, lo:hi], query_view(t)[:, :, lo:hi], shift[t][:], None, ADD)
+
         for t in range(PACK):
             rel_pick = held.tile([P, SLOTS], F32, name="rel_pick%d" % t)
             irr_pick = held.tile([P, SLOTS], F32, name="irr_pick%d" % t)
             rel_terms = held.tile([P, SLOTS], F32, name="rel_terms%d" % t)
-            irr_terms = held.tile([P, SLOTS], F32, name="irr_terms%d" % t)
             rel_share = held.tile([P, 1], F32, name="rel_share%d" % t)
             shift_t = held.tile([P, 1], F32, name="shift%d" % t)
             shift.append(shift_t)
             nc.vector.tensor_copy(rel_pick[:], rel_rows[t][:].indirect(rel_list[:]))
             nc.scalar.activation(rel_terms[:], rel_pick[:], IDENT, scale=fa_scaled[:, t:t + 1], accum_out=rel_share[:])
             nc.vector.tensor_copy(irr_pick[:], irr_rows[t][:].indirect(irr_list[:]))
+            if t == 3:
+                add_shift_vector(2, 0, 2)
+                add_shift_scalar(2, 2, 4)
+            irr_terms = held.tile([P, SLOTS], F32, name="irr_terms%d" % t,
+                                  tag="query_slot2" if t == 3 else "irr_terms%d" % t)
             nc.scalar.activation(irr_terms[:], irr_pick[:], IDENT, scale=fb_scaled[:, t:t + 1], bias=rel_share[:],
                                  accum_out=shift_t[:])
             if t < 2:
-                nc.scalar.activation(x_view[:, t], query_view(t), IDENT, bias=shift_t[:])
+                add_shift_scalar(t, 0, PACK)
 
+        cand_scale = held.tile([P, G], U8, name="cand_scale", tag="irr_slot1", align_bytes=64)
+        nc.gpsimd.memset(cand_scale[:].bitcast(I32), 0)
+        for quad in range(4):
+            nc.sync.dma_start(cand_scale[32 * quad:32 * quad + 4, :].bitcast(I32),
+                              picked_scale[112 + 4 * quad:116 + 4 * quad, :].bitcast(I32))
         nc.vector.tensor_copy(cand_code[0][:], words_all[:].indirect(cand_list[:, 0:HALF // 16]))
-        for t in (2, 3):
-            nc.vector.tensor_scalar(x_view[:, t, :, 0:3], query_view(t)[:, :, 0:3], shift[t][:], None, ADD)
-            nc.scalar.activation(x_view[:, t, :, 3], query_view(t)[:, :, 3], IDENT, bias=shift[t][:])
+        for r in (0, 1):
+            add_shift_vector(3, r, r + 1)
+        for r in (2, 3):
+            add_shift_scalar(3, r, r + 1)
 
         x_code = held.tile([P, Q], U32, name="x_code", align_bytes=64)
         x_scale = held.tile([P, Q], U8, name="x_scale", align_bytes=64)
@@ -114,6 +126,7 @@ def tile_attend_rocchio_pl_kernel(tc, query, rel, irr, fa, fb, cand_words, cand_
             cols = slice(r * P, (r + 1) * P)
             nc.vector.quantize_mx(out=x_code[:, cols].bitcast(FP8X4), scales=x_scale[:, cols],
                                   in_=x_bf[:, r].rearrange("p s t -> p (s t)"))
+        cand_code.append(held.tile([P, HALF], U16, name="cand_code1", tag="x_slot", align_bytes=64))
         nc.vector.tensor_copy(cand_code[1][:], words_all[:].indirect(cand_list[:, HALF // 16:G // 16]))
 
         y_code = held.tile([P, G], U32, name="y_code", align_bytes=64)
@@ -122,26 +135,51 @@ def tile_attend_rocchio_pl_kernel(tc, query, rel, irr, fa, fb, cand_words, cand_
         out1_v = out_1[0].rearrange("p c t -> p (c t)").bitcast(I32)
         out2_v = out_2[0].bitcast(I32)
         y_half = [held.tile([P, PACK, HALF], F32, name="y_half%d" % h) for h in range(2)]
-        for c in range(CHUNKS):
-            h, local = divmod(c * CHUNK, HALF)
-            cols = slice(c * CHUNK, (c + 1) * CHUNK)
-            bank = psum.tile([P, PACK, CHUNK], F32, name="bank%d" % c)
-            for r in range(PACK):
-                rows = slice(r * P, (r + 1) * P)
-                nc.tensor.matmul_mx(out=bank[:, r, :], lhsT=x_code[:, rows].bitcast(FP8X4), lhsT_scale=x_scale[:, rows],
-                                    rhs=cand_code[h][:, local:local + CHUNK].bitcast(FP4X4), rhs_scale=cand_scale[:, cols],
-                                    start=True, stop=True)
-            y_chunk = y_half[h][:, :, local:local + CHUNK]
-            nc.scalar.copy(y_chunk, bank[:])
-            y_bf = held.tile([P, CHUNK, PACK], BF16, name="y_bf%d" % c, align_bytes=64)
-            nc.vector.tensor_copy(y_bf[:].rearrange("p (c i) r -> p c r i", i=4),
-                                  y_chunk.rearrange("p r (c i) -> p c r i", i=4))
-            nc.vector.quantize_mx(out=y_code[:, cols].bitcast(FP8X4), scales=y_scale[:, cols],
-                                  in_=y_bf[:].rearrange("p g r -> p (g r)"))
-            if local + CHUNK == HALF:
-                half_cols = slice(h * HALF, (h + 1) * HALF)
-                nc.sync.dma_start(out0_v[:, :, half_cols], y_half[h][:])
-                nc.sync.dma_start(out1_v[:, half_cols], y_code[:, half_cols].bitcast(I32))
+        y_bf = [held.tile([P, HALF, PACK], BF16, name="y_bf%d" % h, align_bytes=64) for h in range(2)]
+        def multiply(target, r, h, lo, width):
+            rows = slice(r * P, (r + 1) * P)
+            nc.tensor.matmul_mx(out=target, lhsT=x_code[:, rows].bitcast(FP8X4), lhsT_scale=x_scale[:, rows],
+                                rhs=cand_code[h][:, lo:lo + width].bitcast(FP4X4),
+                                rhs_scale=cand_scale[:, h * HALF + lo:h * HALF + lo + width], start=True, stop=True)
+
+        def interleave(h, lo):
+            nc.vector.tensor_copy(y_bf[h][:, lo:lo + CHUNK, :].rearrange("p (c i) r -> p c r i", i=4),
+                                  y_half[h][:, :, lo:lo + CHUNK].rearrange("p r (c i) -> p c r i", i=4))
+
+        def quantise(h):
+            for lo in range(0, HALF, CHUNK):
+                part = slice(h * HALF + lo, h * HALF + lo + CHUNK)
+                nc.vector.quantize_mx(out=y_code[:, part].bitcast(FP8X4), scales=y_scale[:, part],
+                                      in_=y_bf[h][:, lo:lo + CHUNK, :].rearrange("p g r -> p (g r)"))
+            half_cols = slice(h * HALF, (h + 1) * HALF)
+            nc.sync.dma_start(out1_v[:, half_cols], y_code[:, half_cols].bitcast(I32))
+
+        def row_pass(h, r):
+            bank = psum.tile([P, HALF], F32, name="row_bank%d_%d" % (h, r))
+            multiply(bank[:], r, h, 0, HALF)
+            nc.scalar.copy(y_half[h][:, r, :], bank[:])
+
+        def store_rows(h, r):
+            nc.sync.dma_start(out0_v[:, r:r + 2, h * HALF:(h + 1) * HALF], y_half[h][:, r:r + 2, :])
+
+        for r in range(PACK):
+            row_pass(0, r)
+            if r % 2 == 1:
+                store_rows(0, r - 1)
+        for lo in range(0, HALF, CHUNK):
+            interleave(0, lo)
+        quantise(0)
+        for r in (0, 1):
+            row_pass(1, r)
+        store_rows(1, 0)
+        for lo in range(0, HALF, CHUNK):
+            bank = psum.tile([P, 2, CHUNK], F32, name="chunk_bank%d" % lo)
+            for e in range(2):
+                multiply(bank[:, e, :], 2 + e, 1, lo, CHUNK)
+            nc.scalar.copy(y_half[1][:, 2:4, lo:lo + CHUNK], bank[:])
+            interleave(1, lo)
+        store_rows(1, 2)
+        quantise(1)
         for quad in range(4):
             queue = nc.sync if quad % 2 == 0 else nc.scalar
             queue.dma_start(out2_v[4 * quad:4 * quad + 4, :], y_scale[32 * quad:32 * quad + 4, :].bitcast(I32))

@@ -9,6 +9,7 @@ PACK = 4
 CHUNK = 128
 CHUNKS = G // CHUNK
 HALF = G // 2
+ORDER = (0, 2, 1, 3)
 
 FLOPS = 2 * D * Q * G
 
@@ -36,7 +37,8 @@ def tile_attend_rocchio_pl_kernel(tc, query, rel, irr, fa, fb, cand_words, cand_
         cand_list = held.tile([P, G // 16], U16, name="cand_list")
         rel_rows = [held.tile([P, T], F32, name="rel_rows%d" % t) for t in range(PACK)]
         irr_rows = [held.tile([P, T], F32, name="irr_rows%d" % t, tag="irr_slot%d" % t, align_bytes=64) for t in range(PACK)]
-        query_rows = [held.tile([P, Q], F32, name="query_rows%d" % t, tag="query_slot%d" % t) for t in range(PACK)]
+        query_rows = [held.tile([P, Q], F32, name="query_rows%d" % t, tag="query_slot%d" % t, align_bytes=64)
+                      for t in range(PACK)]
         words_all = held.tile([P, U], U16, name="words_all")
         scales_all = held.tile([P, U], U8, name="scales_all")
         fa_sb = held.tile([P, PACK], F32, name="fa_sb")
@@ -52,23 +54,23 @@ def tile_attend_rocchio_pl_kernel(tc, query, rel, irr, fa, fb, cand_words, cand_
         picked_scale = held.tile([P, G], U8, name="picked_scale")
         nc.vector.memset(scales_all[0:112, :].bitcast(I32), 0)
 
+        first, second, third, last = ORDER
         nc.sync.dma_start(cand_list[:], offs3)
         nc.scalar.dma_start(scales_all[112:128, :].bitcast(I32), scales_v)
-        nc.sync.dma_start(rel_rows[0][:], rel_v[:, 0, :])
+        nc.sync.dma_start(rel_rows[first][:], rel_v[:, first, :])
         nc.scalar.dma_start(fa_sb[:], fa.rearrange("(p t) o -> p (t o)", t=PACK))
         nc.scalar.dma_start(fb_sb[:], fb.rearrange("(p t) o -> p (t o)", t=PACK))
         nc.sync.dma_start(rel_list[:], offs)
-        nc.sync.dma_start(irr_rows[0][:], irr_v[:, 0, :])
+        nc.sync.dma_start(irr_rows[first][:], irr_v[:, first, :])
         nc.sync.dma_start(irr_list[:], offs2)
-        nc.sync.dma_start(query_rows[0][:], query_v[:, 0, :])
-        for t in range(1, PACK):
+        for before, t in ((first, second), (second, third), (None, last)):
             nc.sync.dma_start(rel_rows[t][:], rel_v[:, t, :])
+            if before is not None:
+                nc.sync.dma_start(query_rows[before][:], query_v[:, before, :])
             nc.sync.dma_start(irr_rows[t][:], irr_v[:, t, :])
-            if t == 1:
-                nc.sync.dma_start(query_rows[1][:], query_v[:, 1, :])
-        nc.sync.dma_start(query_rows[2][:], query_v[:, 2, :])
+        nc.sync.dma_start(query_rows[third][:], query_v[:, third, :])
         nc.sync.dma_start(words_all[:].bitcast(I32), cand_words[0].bitcast(I32))
-        nc.sync.dma_start(query_rows[3][:], query_v[:, 3, :])
+        nc.sync.dma_start(query_rows[last][:], query_v[:, last, :])
 
         nc.scalar.activation(fa_scaled[:], fa_sb[:], IDENT, scale=1.0 / (SLOTS * SLOTS))
         nc.scalar.activation(fb_scaled[:], fb_sb[:], IDENT, scale=-1.0 / SLOTS)
@@ -76,9 +78,9 @@ def tile_attend_rocchio_pl_kernel(tc, query, rel, irr, fa, fb, cand_words, cand_
         cand_code = [held.tile([P, HALF], U16, name="cand_code0", align_bytes=64)]
         nc.vector.tensor_copy(picked_scale[:], scales_all[:].indirect(cand_list[:]))
 
-        x_bf = held.tile([P, PACK, P, PACK], BF16, name="x_bf", tag="x_slot", align_bytes=64)
+        x_bf = held.tile([P, PACK, P, PACK], BF16, name="x_bf", align_bytes=64)
         x_view = x_bf[:].rearrange("p r s t -> p t s r")
-        shift = []
+        shift = {}
 
         def query_view(t):
             return query_rows[t][:].rearrange("p (s r) -> p s r", r=PACK)
@@ -89,44 +91,44 @@ def tile_attend_rocchio_pl_kernel(tc, query, rel, irr, fa, fb, cand_words, cand_
         def add_shift_vector(t, lo, hi):
             nc.vector.tensor_scalar(x_view[:, t, :, lo:hi], query_view(t)[:, :, lo:hi], shift[t][:], None, ADD)
 
-        for t in range(PACK):
+        for t in ORDER:
             rel_pick = held.tile([P, SLOTS], F32, name="rel_pick%d" % t)
             irr_pick = held.tile([P, SLOTS], F32, name="irr_pick%d" % t)
-            rel_terms = held.tile([P, SLOTS], F32, name="rel_terms%d" % t)
+            slot = {second: "query_slot%d" % first, third: "query_slot%d" % second}.get(t, "rel_terms%d" % t)
+            rel_terms = held.tile([P, SLOTS], F32, name="rel_terms%d" % t, tag=slot, align_bytes=64)
             rel_share = held.tile([P, 1], F32, name="rel_share%d" % t)
             shift_t = held.tile([P, 1], F32, name="shift%d" % t)
-            shift.append(shift_t)
+            shift[t] = shift_t
             nc.vector.tensor_copy(rel_pick[:], rel_rows[t][:].indirect(rel_list[:]))
             nc.scalar.activation(rel_terms[:], rel_pick[:], IDENT, scale=fa_scaled[:, t:t + 1], accum_out=rel_share[:])
             nc.vector.tensor_copy(irr_pick[:], irr_rows[t][:].indirect(irr_list[:]))
-            if t == 3:
-                add_shift_vector(2, 0, 2)
-                add_shift_scalar(2, 2, 4)
-            irr_terms = held.tile([P, SLOTS], F32, name="irr_terms%d" % t,
-                                  tag="query_slot2" if t == 3 else "irr_terms%d" % t)
+            irr_terms = held.tile([P, SLOTS], F32, name="irr_terms%d" % t)
             nc.scalar.activation(irr_terms[:], irr_pick[:], IDENT, scale=fb_scaled[:, t:t + 1], bias=rel_share[:],
                                  accum_out=shift_t[:])
-            if t < 2:
+            if t in (first, second):
                 add_shift_scalar(t, 0, PACK)
+        add_shift_vector(third, 0, 2)
+        add_shift_scalar(third, 2, 4)
 
-        cand_scale = held.tile([P, G], U8, name="cand_scale", tag="irr_slot1", align_bytes=64)
+        cand_scale = held.tile([P, G], U8, name="cand_scale", tag="irr_slot%d" % second, align_bytes=64)
         nc.gpsimd.memset(cand_scale[:].bitcast(I32), 0)
         for quad in range(4):
             nc.sync.dma_start(cand_scale[32 * quad:32 * quad + 4, :].bitcast(I32),
                               picked_scale[112 + 4 * quad:116 + 4 * quad, :].bitcast(I32))
         nc.vector.tensor_copy(cand_code[0][:], words_all[:].indirect(cand_list[:, 0:HALF // 16]))
-        for r in (0, 1):
-            add_shift_vector(3, r, r + 1)
-        for r in (2, 3):
-            add_shift_scalar(3, r, r + 1)
+        add_shift_scalar(last, 3, 4)
+        add_shift_vector(last, 0, 1)
+        add_shift_vector(last, 1, 2)
 
         x_code = held.tile([P, Q], U32, name="x_code", align_bytes=64)
         x_scale = held.tile([P, Q], U8, name="x_scale", align_bytes=64)
-        for r in range(PACK):
+        for r in (0, 1, 3, 2):
+            if r == 3:
+                add_shift_vector(last, 2, 3)
             cols = slice(r * P, (r + 1) * P)
             nc.vector.quantize_mx(out=x_code[:, cols].bitcast(FP8X4), scales=x_scale[:, cols],
                                   in_=x_bf[:, r].rearrange("p s t -> p (s t)"))
-        cand_code.append(held.tile([P, HALF], U16, name="cand_code1", tag="x_slot", align_bytes=64))
+        cand_code.append(held.tile([P, HALF], U16, name="cand_code1", tag="query_slot3", align_bytes=64))
         nc.vector.tensor_copy(cand_code[1][:], words_all[:].indirect(cand_list[:, HALF // 16:G // 16]))
 
         y_code = held.tile([P, G], U32, name="y_code", align_bytes=64)
@@ -155,17 +157,17 @@ def tile_attend_rocchio_pl_kernel(tc, query, rel, irr, fa, fb, cand_words, cand_
             nc.sync.dma_start(out1_v[:, half_cols], y_code[:, half_cols].bitcast(I32))
 
         def row_pass(h, r):
-            bank = psum.tile([P, HALF], F32, name="row_bank%d_%d" % (h, r))
+            bank = psum.tile([P, HALF], F32, name="row_bank%d_%d" % (h, r), tag="row_bank%d_%d" % (h, r))
             multiply(bank[:], r, h, 0, HALF)
             nc.scalar.copy(y_half[h][:, r, :], bank[:])
 
         def store_rows(h, r):
             nc.sync.dma_start(out0_v[:, r:r + 2, h * HALF:(h + 1) * HALF], y_half[h][:, r:r + 2, :])
 
-        for r in range(PACK):
+        for r in (0, 1, 3, 2):
             row_pass(0, r)
-            if r % 2 == 1:
-                store_rows(0, r - 1)
+            if r in (1, 2):
+                store_rows(0, r - r % 2)
         for lo in range(0, HALF, CHUNK):
             interleave(0, lo)
         quantise(0)
@@ -173,10 +175,16 @@ def tile_attend_rocchio_pl_kernel(tc, query, rel, irr, fa, fb, cand_words, cand_
             row_pass(1, r)
         store_rows(1, 0)
         for lo in range(0, HALF, CHUNK):
-            bank = psum.tile([P, 2, CHUNK], F32, name="chunk_bank%d" % lo)
-            for e in range(2):
-                multiply(bank[:, e, :], 2 + e, 1, lo, CHUNK)
-            nc.scalar.copy(y_half[1][:, 2:4, lo:lo + CHUNK], bank[:])
+            if lo == 0:
+                bank = psum.tile([P, 2, CHUNK], F32, name="chunk_bank")
+                for e in range(2):
+                    multiply(bank[:, e, :], 2 + e, 1, lo, CHUNK)
+                nc.scalar.copy(y_half[1][:, 2:4, lo:lo + CHUNK], bank[:])
+            else:
+                for r in (2, 3):
+                    bank = psum.tile([P, CHUNK], F32, name="last_bank%d" % r, tag="row_bank0_%d" % (r - 2))
+                    multiply(bank[:], r, 1, lo, CHUNK)
+                    nc.scalar.copy(y_half[1][:, r, lo:lo + CHUNK], bank[:])
             interleave(1, lo)
         store_rows(1, 2)
         quantise(1)

@@ -10,6 +10,7 @@ CHUNK = 128
 CHUNKS = G // CHUNK
 HALF = G // 2
 ORDER = (0, 2, 1, 3)
+CUT = 96
 
 FLOPS = 2 * D * Q * G
 
@@ -35,9 +36,10 @@ def tile_attend_rocchio_pl_kernel(tc, query, rel, irr, fa, fb, cand_words, cand_
         rel_list = held.tile([P, SLOTS // 16], U16, name="rel_list")
         irr_list = held.tile([P, SLOTS // 16], U16, name="irr_list")
         cand_list = held.tile([P, G // 16], U16, name="cand_list")
-        rel_rows = [held.tile([P, T], F32, name="rel_rows%d" % t) for t in range(PACK)]
-        irr_rows = [held.tile([P, T], F32, name="irr_rows%d" % t, tag="irr_slot%d" % t, align_bytes=64) for t in range(PACK)]
-        query_rows = [held.tile([P, Q], F32, name="query_rows%d" % t, tag="query_slot%d" % t, align_bytes=64)
+        rel_rows = [held.tile([P, T], F32, name="rel_rows%d" % t, tag="rel_slot%d" % t, align_bytes=64)
+                    for t in range(PACK)]
+        irr_rows = [held.tile([P, T], F32, name="irr_rows%d" % t) for t in range(PACK)]
+        query_rows = [held.tile([P, PACK * CUT + SLOTS if t == ORDER[2] else Q], F32, name="query_rows%d" % t, tag="query_slot%d" % t, align_bytes=64)
                       for t in range(PACK)]
         words_all = held.tile([P, U], U16, name="words_all")
         scales_all = held.tile([P, U], U8, name="scales_all")
@@ -68,7 +70,7 @@ def tile_attend_rocchio_pl_kernel(tc, query, rel, irr, fa, fb, cand_words, cand_
             if before is not None:
                 nc.sync.dma_start(query_rows[before][:], query_v[:, before, :])
             nc.sync.dma_start(irr_rows[t][:], irr_v[:, t, :])
-        nc.sync.dma_start(query_rows[third][:], query_v[:, third, :])
+        nc.sync.dma_start(query_rows[third][:, 0:Q], query_v[:, third, :])
         nc.sync.dma_start(words_all[:].bitcast(I32), cand_words[0].bitcast(I32))
         nc.sync.dma_start(query_rows[last][:], query_v[:, last, :])
 
@@ -102,29 +104,39 @@ def tile_attend_rocchio_pl_kernel(tc, query, rel, irr, fa, fb, cand_words, cand_
             nc.vector.tensor_copy(rel_pick[:], rel_rows[t][:].indirect(rel_list[:]))
             nc.scalar.activation(rel_terms[:], rel_pick[:], IDENT, scale=fa_scaled[:, t:t + 1], accum_out=rel_share[:])
             nc.vector.tensor_copy(irr_pick[:], irr_rows[t][:].indirect(irr_list[:]))
-            irr_terms = held.tile([P, SLOTS], F32, name="irr_terms%d" % t)
-            nc.scalar.activation(irr_terms[:], irr_pick[:], IDENT, scale=fb_scaled[:, t:t + 1], bias=rel_share[:],
+            if t == last:
+                nc.vector.tensor_scalar(
+                    x_bf[:].rearrange("p (a b) s t -> p t a s b", a=2)[:, third, :, 0:CUT, :],
+                    query_rows[third][:, 0:PACK * CUT].rearrange("p (s a b) -> p a s b", a=2, b=2),
+                    shift[third][:], None, ADD)
+                nc.scalar.activation(x_view[:, third, CUT:P, :],
+                                     query_rows[third][:, PACK * CUT:Q].rearrange("p (s r) -> p s r", r=PACK),
+                                     IDENT, bias=shift[third][:])
+                irr_terms = query_rows[third][:, PACK * CUT:PACK * CUT + SLOTS]
+            else:
+                irr_terms = held.tile([P, SLOTS], F32, name="irr_terms%d" % t)[:]
+            nc.scalar.activation(irr_terms, irr_pick[:], IDENT, scale=fb_scaled[:, t:t + 1], bias=rel_share[:],
                                  accum_out=shift_t[:])
-            if t in (first, second):
+            if t == first:
+                add_shift_scalar(t, 1, PACK)
+                add_shift_vector(t, 0, 1)
+            if t == second:
                 add_shift_scalar(t, 0, PACK)
-        add_shift_vector(third, 0, 2)
-        add_shift_scalar(third, 2, 4)
 
-        cand_scale = held.tile([P, G], U8, name="cand_scale", tag="irr_slot%d" % second, align_bytes=64)
-        nc.gpsimd.memset(cand_scale[:].bitcast(I32), 0)
+        cand_scale = held.tile([P, G], U8, name="cand_scale", tag="rel_slot%d" % third, align_bytes=64)
+        nc.vector.memset(cand_scale[:].bitcast(I32), 0)
         for quad in range(4):
             nc.sync.dma_start(cand_scale[32 * quad:32 * quad + 4, :].bitcast(I32),
                               picked_scale[112 + 4 * quad:116 + 4 * quad, :].bitcast(I32))
         nc.vector.tensor_copy(cand_code[0][:], words_all[:].indirect(cand_list[:, 0:HALF // 16]))
         add_shift_scalar(last, 3, 4)
+        add_shift_scalar(last, 2, 3)
         add_shift_vector(last, 0, 1)
         add_shift_vector(last, 1, 2)
 
         x_code = held.tile([P, Q], U32, name="x_code", align_bytes=64)
         x_scale = held.tile([P, Q], U8, name="x_scale", align_bytes=64)
         for r in (0, 1, 3, 2):
-            if r == 3:
-                add_shift_vector(last, 2, 3)
             cols = slice(r * P, (r + 1) * P)
             nc.vector.quantize_mx(out=x_code[:, cols].bitcast(FP8X4), scales=x_scale[:, cols],
                                   in_=x_bf[:, r].rearrange("p s t -> p (s t)"))

@@ -105,10 +105,10 @@ def tile_attend_rocchio_pl_kernel(tc, query, rel, irr, fa, fb, cand_words, cand_
             nc.scalar.activation(rel_terms[:], rel_pick[:], IDENT, scale=fa_scaled[:, t:t + 1], accum_out=rel_share[:])
             nc.vector.tensor_copy(irr_pick[:], irr_rows[t][:].indirect(irr_list[:]))
             if t == last:
-                nc.vector.tensor_scalar(
-                    x_bf[:].rearrange("p (a b) s t -> p t a s b", a=2)[:, third, :, 0:CUT, :],
-                    query_rows[third][:, 0:PACK * CUT].rearrange("p (s a b) -> p a s b", a=2, b=2),
-                    shift[third][:], None, ADD)
+                early = query_rows[third][:, 0:PACK * CUT].rearrange("p (s r) -> p s r", r=PACK)
+                for lo in (0, 2):
+                    nc.vector.tensor_scalar(x_view[:, third, 0:CUT, lo:lo + 2], early[:, :, lo:lo + 2],
+                                            shift[third][:], None, ADD)
                 nc.scalar.activation(x_view[:, third, CUT:P, :],
                                      query_rows[third][:, PACK * CUT:Q].rearrange("p (s r) -> p s r", r=PACK),
                                      IDENT, bias=shift[third][:])

@@ -165,8 +165,6 @@ def tile_attend_rocchio_pl_kernel(tc, query, rel, irr, fa, fb, cand_words, cand_
                 part = slice(h * HALF + lo, h * HALF + lo + CHUNK)
                 nc.vector.quantize_mx(out=y_code[:, part].bitcast(FP8X4), scales=y_scale[:, part],
                                       in_=y_bf[h][:, lo:lo + CHUNK, :].rearrange("p g r -> p (g r)"))
-            half_cols = slice(h * HALF, (h + 1) * HALF)
-            nc.sync.dma_start(out1_v[:, half_cols], y_code[:, half_cols].bitcast(I32))
 
         def row_pass(h, r):
             bank = psum.tile([P, HALF], F32, name="row_bank%d_%d" % (h, r), tag="row_bank%d_%d" % (h, r))
@@ -176,19 +174,23 @@ def tile_attend_rocchio_pl_kernel(tc, query, rel, irr, fa, fb, cand_words, cand_
         def store_rows(h, r):
             nc.sync.dma_start(out0_v[:, r:r + 2, h * HALF:(h + 1) * HALF], y_half[h][:, r:r + 2, :])
 
-        for r in (0, 1, 3, 2):
+        for r in (0, 1, 3):
             row_pass(0, r)
-            if r in (1, 2):
-                store_rows(0, r - r % 2)
+            if r == 1:
+                store_rows(0, 0)
         for lo in range(0, HALF, CHUNK):
+            bank = psum.tile([P, CHUNK], F32, name="first_bank%d" % lo, tag="row_bank0_2" if lo == 0 else "chunk_bank")
+            multiply(bank[:], 2, 0, lo, CHUNK)
+            nc.scalar.copy(y_half[0][:, 2, lo:lo + CHUNK], bank[:])
             interleave(0, lo)
+        store_rows(0, 2)
         quantise(0)
         for r in (0, 1):
             row_pass(1, r)
         store_rows(1, 0)
         for lo in range(0, HALF, CHUNK):
             if lo == 0:
-                bank = psum.tile([P, 2, CHUNK], F32, name="chunk_bank")
+                bank = psum.tile([P, 2, CHUNK], F32, name="chunk_bank", tag="late_bank")
                 for e in range(2):
                     multiply(bank[:, e, :], 2 + e, 1, lo, CHUNK)
                 nc.scalar.copy(y_half[1][:, 2:4, lo:lo + CHUNK], bank[:])
@@ -200,6 +202,7 @@ def tile_attend_rocchio_pl_kernel(tc, query, rel, irr, fa, fb, cand_words, cand_
             interleave(1, lo)
         store_rows(1, 2)
         quantise(1)
+        nc.sync.dma_start(out1_v, y_code[:].bitcast(I32))
         for quad in range(4):
             queue = nc.sync if quad % 2 == 0 else nc.scalar
             queue.dma_start(out2_v[4 * quad:4 * quad + 4, :], y_scale[32 * quad:32 * quad + 4, :].bitcast(I32))

@@ -6,9 +6,13 @@ D, T, U, Q, G = 512, 1024, 2048, 512, 512
 SLOTS = 512
 P = 128
 PACK = 4
-CHUNK = 128
-CHUNKS = G // CHUNK
+PER_COLUMN = 16
 HALF = G // 2
+CHUNK = 128
+TAIL = 64
+RUN = 4
+SCALE_ROWS = 16
+SCALE_BASE = P - SCALE_ROWS
 ORDER = (0, 2, 1, 3)
 CUT = 96
 
@@ -27,20 +31,20 @@ ADD = mybir.AluOpType.add
 
 
 def tile_attend_rocchio_pl_kernel(tc, query, rel, irr, fa, fb, cand_words, cand_scales, offs, offs2, offs3,
-                                   out_0, out_1, out_2):
+                                       out_0, out_1, out_2):
     nc = tc.nc
+    first, second, third, last = ORDER
     with ExitStack() as ctx:
         held = ctx.enter_context(tc.tile_pool(name="held", bufs=1))
         psum = ctx.enter_context(tc.psum_pool(name="psum", bufs=1))
 
-        rel_list = held.tile([P, SLOTS // 16], U16, name="rel_list")
-        irr_list = held.tile([P, SLOTS // 16], U16, name="irr_list")
-        cand_list = held.tile([P, G // 16], U16, name="cand_list")
-        rel_rows = [held.tile([P, T], F32, name="rel_rows%d" % t, tag="rel_slot%d" % t, align_bytes=64)
-                    for t in range(PACK)]
+        rel_list = held.tile([P, SLOTS // PER_COLUMN], U16, name="rel_list")
+        irr_list = held.tile([P, SLOTS // PER_COLUMN], U16, name="irr_list")
+        cand_list = held.tile([P, G // PER_COLUMN], U16, name="cand_list")
+        rel_rows = [held.tile([P, T], F32, name="rel_rows%d" % t) for t in range(PACK)]
         irr_rows = [held.tile([P, T], F32, name="irr_rows%d" % t) for t in range(PACK)]
-        query_rows = [held.tile([P, PACK * CUT + SLOTS if t == ORDER[2] else Q], F32, name="query_rows%d" % t, tag="query_slot%d" % t, align_bytes=64)
-                      for t in range(PACK)]
+        query_rows = [held.tile([P, PACK * CUT + SLOTS if t == third else Q], F32, name="query_rows%d" % t,
+                                tag="query_slot%d" % t, align_bytes=64) for t in range(PACK)]
         words_all = held.tile([P, U], U16, name="words_all")
         scales_all = held.tile([P, U], U8, name="scales_all")
         fa_sb = held.tile([P, PACK], F32, name="fa_sb")
@@ -51,25 +55,24 @@ def tile_attend_rocchio_pl_kernel(tc, query, rel, irr, fa, fb, cand_words, cand_
         rel_v = rel.rearrange("(p t) c -> p t c", t=PACK)
         irr_v = irr.rearrange("(p t) c -> p t c", t=PACK)
         query_v = query.rearrange("(p t) c -> p t c", t=PACK)
-        scales_v = cand_scales[0].bitcast(I32)
 
         picked_scale = held.tile([P, G], U8, name="picked_scale")
-        nc.vector.memset(scales_all[0:112, :].bitcast(I32), 0)
+        nc.vector.memset(scales_all[0:SCALE_BASE, :].bitcast(I32), 0)
 
-        first, second, third, last = ORDER
         nc.sync.dma_start(cand_list[:], offs3)
-        nc.scalar.dma_start(scales_all[112:128, :].bitcast(I32), scales_v)
+        nc.scalar.dma_start(scales_all[SCALE_BASE:P, :].bitcast(I32), cand_scales[0].bitcast(I32))
         nc.sync.dma_start(rel_rows[first][:], rel_v[:, first, :])
         nc.scalar.dma_start(fa_sb[:], fa.rearrange("(p t) o -> p (t o)", t=PACK))
         nc.scalar.dma_start(fb_sb[:], fb.rearrange("(p t) o -> p (t o)", t=PACK))
         nc.sync.dma_start(rel_list[:], offs)
         nc.sync.dma_start(irr_rows[first][:], irr_v[:, first, :])
         nc.sync.dma_start(irr_list[:], offs2)
-        for before, t in ((first, second), (second, third), (None, last)):
+        for before, t in ((first, second), (second, third)):
             nc.sync.dma_start(rel_rows[t][:], rel_v[:, t, :])
-            if before is not None:
-                nc.sync.dma_start(query_rows[before][:], query_v[:, before, :])
+            nc.sync.dma_start(query_rows[before][:], query_v[:, before, :])
             nc.sync.dma_start(irr_rows[t][:], irr_v[:, t, :])
+        nc.sync.dma_start(rel_rows[last][:], rel_v[:, last, :])
+        nc.sync.dma_start(irr_rows[last][:], irr_v[:, last, :])
         nc.sync.dma_start(query_rows[third][:, 0:Q], query_v[:, third, :])
         nc.sync.dma_start(words_all[:].bitcast(I32), cand_words[0].bitcast(I32))
         nc.sync.dma_start(query_rows[last][:], query_v[:, last, :])
@@ -84,55 +87,57 @@ def tile_attend_rocchio_pl_kernel(tc, query, rel, irr, fa, fb, cand_words, cand_
         x_view = x_bf[:].rearrange("p r s t -> p t s r")
         shift = {}
 
-        def query_view(t):
-            return query_rows[t][:].rearrange("p (s r) -> p s r", r=PACK)
+        def by_group(columns):
+            return columns.rearrange("p (s r) -> p s r", r=PACK)
 
         def add_shift_scalar(t, lo, hi):
-            nc.scalar.activation(x_view[:, t, :, lo:hi], query_view(t)[:, :, lo:hi], IDENT, bias=shift[t][:])
+            nc.scalar.activation(x_view[:, t, :, lo:hi], by_group(query_rows[t][:])[:, :, lo:hi], IDENT,
+                                 bias=shift[t][:])
 
         def add_shift_vector(t, lo, hi):
-            nc.vector.tensor_scalar(x_view[:, t, :, lo:hi], query_view(t)[:, :, lo:hi], shift[t][:], None, ADD)
+            nc.vector.tensor_scalar(x_view[:, t, :, lo:hi], by_group(query_rows[t][:])[:, :, lo:hi], shift[t][:],
+                                    None, ADD)
 
+        terms_slot = {second: "query_slot%d" % first, third: "query_slot%d" % second}
         for t in ORDER:
             rel_pick = held.tile([P, SLOTS], F32, name="rel_pick%d" % t)
             irr_pick = held.tile([P, SLOTS], F32, name="irr_pick%d" % t)
-            slot = {second: "query_slot%d" % first, third: "query_slot%d" % second}.get(t, "rel_terms%d" % t)
-            rel_terms = held.tile([P, SLOTS], F32, name="rel_terms%d" % t, tag=slot, align_bytes=64)
+            rel_terms = held.tile([P, SLOTS], F32, name="rel_terms%d" % t,
+                                  tag=terms_slot.get(t, "rel_terms%d" % t), align_bytes=64)
             rel_share = held.tile([P, 1], F32, name="rel_share%d" % t)
-            shift_t = held.tile([P, 1], F32, name="shift%d" % t)
-            shift[t] = shift_t
+            shift[t] = held.tile([P, 1], F32, name="shift%d" % t)
             nc.vector.tensor_copy(rel_pick[:], rel_rows[t][:].indirect(rel_list[:]))
             nc.scalar.activation(rel_terms[:], rel_pick[:], IDENT, scale=fa_scaled[:, t:t + 1], accum_out=rel_share[:])
             nc.vector.tensor_copy(irr_pick[:], irr_rows[t][:].indirect(irr_list[:]))
             if t == last:
-                early = query_rows[third][:, 0:PACK * CUT].rearrange("p (s r) -> p s r", r=PACK)
+                low_words = by_group(query_rows[third][:, 0:PACK * CUT])
                 for lo in (0, 2):
-                    nc.vector.tensor_scalar(x_view[:, third, 0:CUT, lo:lo + 2], early[:, :, lo:lo + 2],
+                    nc.vector.tensor_scalar(x_view[:, third, 0:CUT, lo:lo + 2], low_words[:, :, lo:lo + 2],
                                             shift[third][:], None, ADD)
-                nc.scalar.activation(x_view[:, third, CUT:P, :],
-                                     query_rows[third][:, PACK * CUT:Q].rearrange("p (s r) -> p s r", r=PACK),
+                nc.scalar.activation(x_view[:, third, CUT:P, :], by_group(query_rows[third][:, PACK * CUT:Q]),
                                      IDENT, bias=shift[third][:])
                 irr_terms = query_rows[third][:, PACK * CUT:PACK * CUT + SLOTS]
             else:
                 irr_terms = held.tile([P, SLOTS], F32, name="irr_terms%d" % t)[:]
             nc.scalar.activation(irr_terms, irr_pick[:], IDENT, scale=fb_scaled[:, t:t + 1], bias=rel_share[:],
-                                 accum_out=shift_t[:])
+                                 accum_out=shift[t][:])
             if t == first:
-                add_shift_scalar(t, 1, PACK)
-                add_shift_vector(t, 0, 1)
+                add_shift_scalar(t, 2, PACK)
+                add_shift_vector(t, 0, 2)
             if t == second:
                 add_shift_scalar(t, 0, PACK)
 
-        cand_scale = held.tile([P, G], U8, name="cand_scale", tag="rel_slot%d" % third, align_bytes=64)
+        cand_scale = held.tile([P, G], U8, name="cand_scale", align_bytes=64)
         nc.vector.memset(cand_scale[:].bitcast(I32), 0)
         for quad in range(4):
-            nc.sync.dma_start(cand_scale[32 * quad:32 * quad + 4, :].bitcast(I32),
-                              picked_scale[112 + 4 * quad:116 + 4 * quad, :].bitcast(I32))
-        nc.vector.tensor_copy(cand_code[0][:], words_all[:].indirect(cand_list[:, 0:HALF // 16]))
-        add_shift_scalar(last, 3, 4)
-        add_shift_scalar(last, 2, 3)
-        add_shift_vector(last, 0, 1)
-        add_shift_vector(last, 1, 2)
+            rows = slice(SCALE_BASE + 4 * quad, SCALE_BASE + 4 * quad + 4)
+            nc.sync.dma_start(cand_scale[32 * quad:32 * quad + 4, :].bitcast(I32), picked_scale[rows, :].bitcast(I32))
+        nc.vector.tensor_copy(cand_code[0][:], words_all[:].indirect(cand_list[:, 0:HALF // PER_COLUMN]))
+
+        for r in (3, 2):
+            add_shift_scalar(last, r, r + 1)
+        for r in (0, 1):
+            add_shift_vector(last, r, r + 1)
 
         x_code = held.tile([P, Q], U32, name="x_code", align_bytes=64)
         x_scale = held.tile([P, Q], U8, name="x_scale", align_bytes=64)
@@ -140,8 +145,8 @@ def tile_attend_rocchio_pl_kernel(tc, query, rel, irr, fa, fb, cand_words, cand_
             cols = slice(r * P, (r + 1) * P)
             nc.vector.quantize_mx(out=x_code[:, cols].bitcast(FP8X4), scales=x_scale[:, cols],
                                   in_=x_bf[:, r].rearrange("p s t -> p (s t)"))
-        cand_code.append(held.tile([P, HALF], U16, name="cand_code1", tag="query_slot3", align_bytes=64))
-        nc.vector.tensor_copy(cand_code[1][:], words_all[:].indirect(cand_list[:, HALF // 16:G // 16]))
+        cand_code.append(held.tile([P, HALF], U16, name="cand_code1", tag="query_slot%d" % last, align_bytes=64))
+        nc.vector.tensor_copy(cand_code[1][:], words_all[:].indirect(cand_list[:, HALF // PER_COLUMN:G // PER_COLUMN]))
 
         y_code = held.tile([P, G], U32, name="y_code", align_bytes=64)
         y_scale = held.tile([P, G], U8, name="y_scale", align_bytes=64)
@@ -150,58 +155,59 @@ def tile_attend_rocchio_pl_kernel(tc, query, rel, irr, fa, fb, cand_words, cand_
         out2_v = out_2[0].bitcast(I32)
         y_half = [held.tile([P, PACK, HALF], F32, name="y_half%d" % h) for h in range(2)]
         y_bf = [held.tile([P, HALF, PACK], BF16, name="y_bf%d" % h, align_bytes=64) for h in range(2)]
+
         def multiply(target, r, h, lo, width):
             rows = slice(r * P, (r + 1) * P)
             nc.tensor.matmul_mx(out=target, lhsT=x_code[:, rows].bitcast(FP8X4), lhsT_scale=x_scale[:, rows],
                                 rhs=cand_code[h][:, lo:lo + width].bitcast(FP4X4),
                                 rhs_scale=cand_scale[:, h * HALF + lo:h * HALF + lo + width], start=True, stop=True)
 
-        def interleave(h, lo):
-            nc.vector.tensor_copy(y_bf[h][:, lo:lo + CHUNK, :].rearrange("p (c i) r -> p c r i", i=4),
-                                  y_half[h][:, :, lo:lo + CHUNK].rearrange("p r (c i) -> p c r i", i=4))
+        def product(r, h, lo, width, bank_tag):
+            bank = psum.tile([P, width], F32, name="bank%d_%d_%d" % (h, r, lo), tag=bank_tag)
+            multiply(bank[:], r, h, lo, width)
+            nc.scalar.copy(y_half[h][:, r, lo:lo + width], bank[:])
 
-        def quantise(h):
-            for lo in range(0, HALF, CHUNK):
-                part = slice(h * HALF + lo, h * HALF + lo + CHUNK)
-                nc.vector.quantize_mx(out=y_code[:, part].bitcast(FP8X4), scales=y_scale[:, part],
-                                      in_=y_bf[h][:, lo:lo + CHUNK, :].rearrange("p g r -> p (g r)"))
+        def interleave(h, lo, width):
+            nc.vector.tensor_copy(y_bf[h][:, lo:lo + width, :].rearrange("p (c i) r -> p c r i", i=RUN),
+                                  y_half[h][:, :, lo:lo + width].rearrange("p r (c i) -> p c r i", i=RUN))
 
-        def row_pass(h, r):
-            bank = psum.tile([P, HALF], F32, name="row_bank%d_%d" % (h, r), tag="row_bank%d_%d" % (h, r))
-            multiply(bank[:], r, h, 0, HALF)
-            nc.scalar.copy(y_half[h][:, r, :], bank[:])
+        def quantise(h, lo, width):
+            cols = slice(h * HALF + lo, h * HALF + lo + width)
+            nc.vector.quantize_mx(out=y_code[:, cols].bitcast(FP8X4), scales=y_scale[:, cols],
+                                  in_=y_bf[h][:, lo:lo + width, :].rearrange("p g r -> p (g r)"))
 
         def store_rows(h, r):
             nc.sync.dma_start(out0_v[:, r:r + 2, h * HALF:(h + 1) * HALF], y_half[h][:, r:r + 2, :])
 
-        for r in (0, 1, 3):
-            row_pass(0, r)
-            if r == 1:
-                store_rows(0, 0)
-        for lo in range(0, HALF, CHUNK):
-            bank = psum.tile([P, CHUNK], F32, name="first_bank%d" % lo, tag="row_bank0_2" if lo == 0 else "chunk_bank")
-            multiply(bank[:], 2, 0, lo, CHUNK)
-            nc.scalar.copy(y_half[0][:, 2, lo:lo + CHUNK], bank[:])
-            interleave(0, lo)
-        store_rows(0, 2)
-        quantise(0)
         for r in (0, 1):
-            row_pass(1, r)
+            product(r, 0, 0, HALF, "bank%d" % r)
+        store_rows(0, 0)
+        product(3, 0, 0, HALF, "bank2")
+        for c in range(2):
+            product(2, 0, c * CHUNK, CHUNK, "bank%d" % (3 + c))
+            interleave(0, c * CHUNK, CHUNK)
+        store_rows(0, 2)
+        for c in range(2):
+            quantise(0, c * CHUNK, CHUNK)
+
+        for r in (0, 1):
+            product(r, 1, 0, HALF, "bank%d" % (5 + r))
         store_rows(1, 0)
-        for lo in range(0, HALF, CHUNK):
-            if lo == 0:
-                bank = psum.tile([P, 2, CHUNK], F32, name="chunk_bank", tag="late_bank")
-                for e in range(2):
-                    multiply(bank[:, e, :], 2 + e, 1, lo, CHUNK)
-                nc.scalar.copy(y_half[1][:, 2:4, lo:lo + CHUNK], bank[:])
-            else:
-                for r in (2, 3):
-                    bank = psum.tile([P, CHUNK], F32, name="last_bank%d" % r, tag="row_bank0_%d" % (r - 2))
-                    multiply(bank[:], r, 1, lo, CHUNK)
-                    nc.scalar.copy(y_half[1][:, r, lo:lo + CHUNK], bank[:])
-            interleave(1, lo)
+        pair_bank = psum.tile([P, 2, CHUNK], F32, name="pair_bank", tag="bank7")
+        for e in range(2):
+            multiply(pair_bank[:, e, :], 2 + e, 1, 0, CHUNK)
+        nc.scalar.copy(y_half[1][:, 2:PACK, 0:CHUNK], pair_bank[:])
+        interleave(1, 0, CHUNK)
+        product(2, 1, CHUNK, CHUNK, "bank0")
+        product(3, 1, CHUNK, TAIL, "bank1")
+        product(3, 1, CHUNK + TAIL, TAIL, "bank2")
         store_rows(1, 2)
-        quantise(1)
+        interleave(1, CHUNK, TAIL)
+        quantise(1, 0, CHUNK)
+        interleave(1, CHUNK + TAIL, TAIL)
+        quantise(1, CHUNK, TAIL)
+        quantise(1, CHUNK + TAIL, TAIL)
+
         nc.sync.dma_start(out1_v, y_code[:].bitcast(I32))
         for quad in range(4):
             queue = nc.sync if quad % 2 == 0 else nc.scalar

@@ -121,11 +121,9 @@ def tile_attend_rocchio_pl_kernel(tc, query, rel, irr, fa, fb, cand_words, cand_
                 irr_terms = held.tile([P, SLOTS], F32, name="irr_terms%d" % t)[:]
             nc.scalar.activation(irr_terms, irr_pick[:], IDENT, scale=fb_scaled[:, t:t + 1], bias=rel_share[:],
                                  accum_out=shift[t][:])
-            if t == first:
-                add_shift_scalar(t, 2, PACK)
-                add_shift_vector(t, 0, 2)
-            if t == second:
-                add_shift_scalar(t, 0, PACK)
+            if t in (first, second):
+                add_shift_scalar(t, 1, PACK)
+                add_shift_vector(t, 0, 1)
 
         cand_scale = held.tile([P, G], U8, name="cand_scale", align_bytes=64)
         nc.vector.memset(cand_scale[:].bitcast(I32), 0)

@@ -61,12 +61,12 @@ def tile_attend_rocchio_pl_kernel(tc, query, rel, irr, fa, fb, cand_words, cand_
 
         nc.sync.dma_start(cand_list[:], offs3)
         nc.scalar.dma_start(scales_all[SCALE_BASE:P, :].bitcast(I32), cand_scales[0].bitcast(I32))
+        nc.sync.dma_start(rel_list[:], offs)
+        nc.sync.dma_start(irr_list[:], offs2)
         nc.sync.dma_start(rel_rows[first][:], rel_v[:, first, :])
         nc.scalar.dma_start(fa_sb[:], fa.rearrange("(p t) o -> p (t o)", t=PACK))
         nc.scalar.dma_start(fb_sb[:], fb.rearrange("(p t) o -> p (t o)", t=PACK))
-        nc.sync.dma_start(rel_list[:], offs)
         nc.sync.dma_start(irr_rows[first][:], irr_v[:, first, :])
-        nc.sync.dma_start(irr_list[:], offs2)
         for before, t in ((first, second), (second, third)):
             nc.sync.dma_start(rel_rows[t][:], rel_v[:, t, :])
             nc.sync.dma_start(query_rows[before][:], query_v[:, before, :])
@@ -206,7 +206,6 @@ def tile_attend_rocchio_pl_kernel(tc, query, rel, irr, fa, fb, cand_words, cand_
         quantise(1, CHUNK, TAIL)
         quantise(1, CHUNK + TAIL, TAIL)
 
-        nc.sync.dma_start(out1_v, y_code[:].bitcast(I32))
+        nc.scalar.dma_start(out1_v, y_code[:].bitcast(I32))
         for quad in range(4):
-            queue = nc.sync if quad % 2 == 0 else nc.scalar
-            queue.dma_start(out2_v[4 * quad:4 * quad + 4, :], y_scale[32 * quad:32 * quad + 4, :].bitcast(I32))
+            nc.sync.dma_start(out2_v[4 * quad:4 * quad + 4, :], y_scale[32 * quad:32 * quad + 4, :].bitcast(I32))

@@ -180,10 +180,14 @@ def tile_attend_rocchio_pl_kernel(tc, query, rel, irr, fa, fb, cand_words, cand_
         for r in (0, 1):
             product(r, 0, 0, HALF, "bank%d" % r)
         store_rows(0, 0)
-        product(3, 0, 0, HALF, "bank2")
-        for c in range(2):
-            product(2, 0, c * CHUNK, CHUNK, "bank%d" % (3 + c))
-            interleave(0, c * CHUNK, CHUNK)
+        product(3, 0, 0, CHUNK, "bank2")
+        product(2, 0, 0, CHUNK, "bank3")
+        interleave(0, 0, CHUNK)
+        first_pair = psum.tile([P, 2, CHUNK], F32, name="first_pair", tag="bank4")
+        for e in range(2):
+            multiply(first_pair[:, e, :], 2 + e, 0, CHUNK, CHUNK)
+        nc.scalar.copy(y_half[0][:, 2:PACK, CHUNK:HALF], first_pair[:])
+        interleave(0, CHUNK, CHUNK)
         store_rows(0, 2)
         for c in range(2):
             quantise(0, c * CHUNK, CHUNK)

@@ -122,8 +122,8 @@ def tile_attend_rocchio_pl_kernel(tc, query, rel, irr, fa, fb, cand_words, cand_
             nc.scalar.activation(irr_terms, irr_pick[:], IDENT, scale=fb_scaled[:, t:t + 1], bias=rel_share[:],
                                  accum_out=shift[t][:])
             if t in (first, second):
-                add_shift_scalar(t, 1, PACK)
-                add_shift_vector(t, 0, 1)
+                add_shift_scalar(t, 2, PACK)
+                add_shift_vector(t, 0, 2)
 
         cand_scale = held.tile([P, G], U8, name="cand_scale", align_bytes=64)
         nc.vector.memset(cand_scale[:].bitcast(I32), 0)

@@ -16,6 +16,8 @@ SCALE_BASE = P - SCALE_ROWS
 ORDER = (0, 2, 1, 3)
 CUT = 96
 
+EARLY = {ORDER[0]: 2, ORDER[1]: 1}
+
 FLOPS = 2 * D * Q * G
 
 F32 = mybir.dt.float32
@@ -122,8 +124,8 @@ def tile_attend_rocchio_pl_kernel(tc, query, rel, irr, fa, fb, cand_words, cand_
             nc.scalar.activation(irr_terms, irr_pick[:], IDENT, scale=fb_scaled[:, t:t + 1], bias=rel_share[:],
                                  accum_out=shift[t][:])
             if t in (first, second):
-                add_shift_scalar(t, 2, PACK)
-                add_shift_vector(t, 0, 2)
+                add_shift_scalar(t, EARLY[t], PACK)
+                add_shift_vector(t, 0, EARLY[t])
 
         cand_scale = held.tile([P, G], U8, name="cand_scale", align_bytes=64)
         nc.vector.memset(cand_scale[:].bitcast(I32), 0)

@@ -167,6 +167,12 @@ def tile_attend_rocchio_pl_kernel(tc, query, rel, irr, fa, fb, cand_words, cand_
             multiply(bank[:], r, h, lo, width)
             nc.scalar.copy(y_half[h][:, r, lo:lo + width], bank[:])
 
+        def pair_product(r, h, lo, bank_tag):
+            bank = psum.tile([P, 2, CHUNK], F32, name="pair%d_%d_%d" % (h, r, lo), tag=bank_tag)
+            for e in range(2):
+                multiply(bank[:, e, :], r + e, h, lo, CHUNK)
+            nc.scalar.copy(y_half[h][:, r:r + 2, lo:lo + CHUNK], bank[:])
+
         def interleave(h, lo, width):
             nc.vector.tensor_copy(y_bf[h][:, lo:lo + width, :].rearrange("p (c i) r -> p c r i", i=RUN),
                                   y_half[h][:, :, lo:lo + width].rearrange("p r (c i) -> p c r i", i=RUN))
@@ -185,23 +191,17 @@ def tile_attend_rocchio_pl_kernel(tc, query, rel, irr, fa, fb, cand_words, cand_
         product(3, 0, 0, CHUNK, "bank2")
         product(2, 0, 0, CHUNK, "bank3")
         interleave(0, 0, CHUNK)
-        first_pair = psum.tile([P, 2, CHUNK], F32, name="first_pair", tag="bank4")
-        for e in range(2):
-            multiply(first_pair[:, e, :], 2 + e, 0, CHUNK, CHUNK)
-        nc.scalar.copy(y_half[0][:, 2:PACK, CHUNK:HALF], first_pair[:])
+        pair_product(2, 0, CHUNK, "bank4")
         interleave(0, CHUNK, CHUNK)
         store_rows(0, 2)
         for c in range(2):
             quantise(0, c * CHUNK, CHUNK)
 
-        for r in (0, 1):
-            product(r, 1, 0, HALF, "bank%d" % (5 + r))
-        store_rows(1, 0)
-        pair_bank = psum.tile([P, 2, CHUNK], F32, name="pair_bank", tag="bank7")
-        for e in range(2):
-            multiply(pair_bank[:, e, :], 2 + e, 1, 0, CHUNK)
-        nc.scalar.copy(y_half[1][:, 2:PACK, 0:CHUNK], pair_bank[:])
+        pair_product(0, 1, 0, "bank5")
+        pair_product(2, 1, 0, "bank6")
         interleave(1, 0, CHUNK)
+        pair_product(0, 1, CHUNK, "bank7")
+        store_rows(1, 0)
         product(2, 1, CHUNK, CHUNK, "bank0")
         product(3, 1, CHUNK, TAIL, "bank1")
         product(3, 1, CHUNK + TAIL, TAIL, "bank2")

@@ -13,10 +13,8 @@ TAIL = 64
 RUN = 4
 SCALE_ROWS = 16
 SCALE_BASE = P - SCALE_ROWS
-ORDER = (0, 2, 1, 3)
+ORDER = (1, 2, 0, 3)
 CUT = 96
-
-EARLY = {ORDER[0]: 2, ORDER[1]: 1}
 
 FLOPS = 2 * D * Q * G
 
@@ -29,6 +27,7 @@ U8 = mybir.dt.uint8
 FP8X4 = mybir.dt.float8_e4m3fn_x4
 FP4X4 = mybir.dt.float4_e2m1fn_x4
 IDENT = mybir.ActivationFunctionType.Identity
+COPY = mybir.ActivationFunctionType.Copy
 ADD = mybir.AluOpType.add
 
 
@@ -43,10 +42,15 @@ def tile_attend_rocchio_pl_kernel(tc, query, rel, irr, fa, fb, cand_words, cand_
         rel_list = held.tile([P, SLOTS // PER_COLUMN], U16, name="rel_list")
         irr_list = held.tile([P, SLOTS // PER_COLUMN], U16, name="irr_list")
         cand_list = held.tile([P, G // PER_COLUMN], U16, name="cand_list")
-        rel_rows = [held.tile([P, T], F32, name="rel_rows%d" % t) for t in range(PACK)]
-        irr_rows = [held.tile([P, T], F32, name="irr_rows%d" % t) for t in range(PACK)]
-        query_rows = [held.tile([P, PACK * CUT + SLOTS if t == third else Q], F32, name="query_rows%d" % t,
-                                tag="query_slot%d" % t, align_bytes=64) for t in range(PACK)]
+        rel_pair = held.tile([P, 2, T], F32, name="rel_pair")
+        query_pair = held.tile([P, 2, Q], F32, name="query_pair", align_bytes=64)
+        rel_rows = {first: rel_pair[:, 0, :], second: rel_pair[:, 1, :]}
+        irr_rows = [held.tile([P, T], F32, name="irr_rows%d" % t)[:] for t in range(PACK)]
+        query_rows = {first: query_pair[:, 0, :], second: query_pair[:, 1, :]}
+        for t in (third, last):
+            rel_rows[t] = held.tile([P, T], F32, name="rel_rows%d" % t)[:]
+            query_rows[t] = held.tile([P, PACK * CUT + SLOTS if t == third else Q], F32, name="query_rows%d" % t,
+                                      tag="query_slot%d" % t, align_bytes=64)[:]
         words_all = held.tile([P, U], U16, name="words_all")
         scales_all = held.tile([P, U], U8, name="scales_all")
         fa_sb = held.tile([P, PACK], F32, name="fa_sb")
@@ -65,19 +69,18 @@ def tile_attend_rocchio_pl_kernel(tc, query, rel, irr, fa, fb, cand_words, cand_
         nc.scalar.dma_start(scales_all[SCALE_BASE:P, :].bitcast(I32), cand_scales[0].bitcast(I32))
         nc.sync.dma_start(rel_list[:], offs)
         nc.sync.dma_start(irr_list[:], offs2)
-        nc.sync.dma_start(rel_rows[first][:], rel_v[:, first, :])
+        nc.sync.dma_start(rel_pair[:], rel_v[:, first:second + 1, :])
         nc.scalar.dma_start(fa_sb[:], fa.rearrange("(p t) o -> p (t o)", t=PACK))
         nc.scalar.dma_start(fb_sb[:], fb.rearrange("(p t) o -> p (t o)", t=PACK))
-        nc.sync.dma_start(irr_rows[first][:], irr_v[:, first, :])
-        for before, t in ((first, second), (second, third)):
-            nc.sync.dma_start(rel_rows[t][:], rel_v[:, t, :])
-            nc.sync.dma_start(query_rows[before][:], query_v[:, before, :])
-            nc.sync.dma_start(irr_rows[t][:], irr_v[:, t, :])
-        nc.sync.dma_start(rel_rows[last][:], rel_v[:, last, :])
-        nc.sync.dma_start(irr_rows[last][:], irr_v[:, last, :])
+        for t in (first, second):
+            nc.sync.dma_start(irr_rows[t], irr_v[:, t, :])
+        nc.sync.dma_start(query_pair[:], query_v[:, first:second + 1, :])
+        for t in (third, last):
+            nc.sync.dma_start(rel_rows[t], rel_v[:, t, :])
+            nc.sync.dma_start(irr_rows[t], irr_v[:, t, :])
         nc.sync.dma_start(query_rows[third][:, 0:Q], query_v[:, third, :])
         nc.sync.dma_start(words_all[:].bitcast(I32), cand_words[0].bitcast(I32))
-        nc.sync.dma_start(query_rows[last][:], query_v[:, last, :])
+        nc.sync.dma_start(query_rows[last], query_v[:, last, :])
 
         nc.scalar.activation(fa_scaled[:], fa_sb[:], IDENT, scale=1.0 / (SLOTS * SLOTS))
         nc.scalar.activation(fb_scaled[:], fb_sb[:], IDENT, scale=-1.0 / SLOTS)
@@ -93,24 +96,41 @@ def tile_attend_rocchio_pl_kernel(tc, query, rel, irr, fa, fb, cand_words, cand_
             return columns.rearrange("p (s r) -> p s r", r=PACK)
 
         def add_shift_scalar(t, lo, hi):
-            nc.scalar.activation(x_view[:, t, :, lo:hi], by_group(query_rows[t][:])[:, :, lo:hi], IDENT,
+            nc.scalar.activation(x_view[:, t, :, lo:hi], by_group(query_rows[t])[:, :, lo:hi], IDENT,
                                  bias=shift[t][:])
 
         def add_shift_vector(t, lo, hi):
-            nc.vector.tensor_scalar(x_view[:, t, :, lo:hi], by_group(query_rows[t][:])[:, :, lo:hi], shift[t][:],
+            nc.vector.tensor_scalar(x_view[:, t, :, lo:hi], by_group(query_rows[t])[:, :, lo:hi], shift[t][:],
                                     None, ADD)
 
-        terms_slot = {second: "query_slot%d" % first, third: "query_slot%d" % second}
-        for t in ORDER:
+        picks, shares = {}, {}
+        for t in (first, second):
+            picks[t] = [held.tile([P, SLOTS], F32, name="%s_pick%d" % (side, t)) for side in ("rel", "irr")]
+            shares[t] = held.tile([P, 1], F32, name="rel_share%d" % t)
+            shift[t] = held.tile([P, 1], F32, name="shift%d" % t)
+        nc.vector.tensor_copy(picks[first][0][:], rel_rows[first].indirect(rel_list[:]))
+        nc.scalar.activation(picks[second][0][:], rel_rows[second].indirect(rel_list[:]), COPY)
+        for t in (first, second):
+            rel_terms = held.tile([P, SLOTS], F32, name="rel_terms%d" % t)
+            nc.scalar.activation(rel_terms[:], picks[t][0][:], IDENT, scale=fa_scaled[:, t:t + 1],
+                                 accum_out=shares[t][:])
+        for t in (first, second):
+            nc.vector.tensor_copy(picks[t][1][:], irr_rows[t].indirect(irr_list[:]))
+            irr_terms = held.tile([P, SLOTS], F32, name="irr_terms%d" % t)
+            nc.scalar.activation(irr_terms[:], picks[t][1][:], IDENT, scale=fb_scaled[:, t:t + 1],
+                                 bias=shares[t][:], accum_out=shift[t][:])
+        for lo in (0, 2):
+            add_shift_vector(first, lo, lo + 2)
+        add_shift_scalar(second, 0, PACK)
+        for t in (third, last):
             rel_pick = held.tile([P, SLOTS], F32, name="rel_pick%d" % t)
             irr_pick = held.tile([P, SLOTS], F32, name="irr_pick%d" % t)
-            rel_terms = held.tile([P, SLOTS], F32, name="rel_terms%d" % t,
-                                  tag=terms_slot.get(t, "rel_terms%d" % t), align_bytes=64)
+            rel_terms = held.tile([P, SLOTS], F32, name="rel_terms%d" % t)
             rel_share = held.tile([P, 1], F32, name="rel_share%d" % t)
             shift[t] = held.tile([P, 1], F32, name="shift%d" % t)
-            nc.vector.tensor_copy(rel_pick[:], rel_rows[t][:].indirect(rel_list[:]))
+            nc.vector.tensor_copy(rel_pick[:], rel_rows[t].indirect(rel_list[:]))
             nc.scalar.activation(rel_terms[:], rel_pick[:], IDENT, scale=fa_scaled[:, t:t + 1], accum_out=rel_share[:])
-            nc.vector.tensor_copy(irr_pick[:], irr_rows[t][:].indirect(irr_list[:]))
+            nc.vector.tensor_copy(irr_pick[:], irr_rows[t].indirect(irr_list[:]))
             if t == last:
                 low_words = by_group(query_rows[third][:, 0:PACK * CUT])
                 for lo in (0, 2):
@@ -123,9 +143,6 @@ def tile_attend_rocchio_pl_kernel(tc, query, rel, irr, fa, fb, cand_words, cand_
                 irr_terms = held.tile([P, SLOTS], F32, name="irr_terms%d" % t)[:]
             nc.scalar.activation(irr_terms, irr_pick[:], IDENT, scale=fb_scaled[:, t:t + 1], bias=rel_share[:],
                                  accum_out=shift[t][:])
-            if t in (first, second):
-                add_shift_scalar(t, EARLY[t], PACK)
-                add_shift_vector(t, 0, EARLY[t])
 
         cand_scale = held.tile([P, G], U8, name="cand_scale", align_bytes=64)
         nc.vector.memset(cand_scale[:].bitcast(I32), 0)

from contextlib import ExitStack

import concourse.mybir as mybir

D, T, U, Q, G = 512, 1024, 2048, 512, 512
SLOTS = 512
P = 128
PACK = 4
PER_COLUMN = 16
HALF = G // 2
CHUNK = 128
TAIL = 64
RUN = 4
SCALE_ROWS = 16
SCALE_BASE = P - SCALE_ROWS
ORDER = (1, 2, 0, 3)
CUT = 96

FLOPS = 2 * D * Q * G

F32 = mybir.dt.float32
BF16 = mybir.dt.bfloat16
I32 = mybir.dt.int32
U32 = mybir.dt.uint32
U16 = mybir.dt.uint16
U8 = mybir.dt.uint8
FP8X4 = mybir.dt.float8_e4m3fn_x4
FP4X4 = mybir.dt.float4_e2m1fn_x4
IDENT = mybir.ActivationFunctionType.Identity
COPY = mybir.ActivationFunctionType.Copy
ADD = mybir.AluOpType.add


def tile_attend_rocchio_pl_kernel(tc, query, rel, irr, fa, fb, cand_words, cand_scales, offs, offs2, offs3,
                                       out_0, out_1, out_2):
    nc = tc.nc
    first, second, third, last = ORDER
    with ExitStack() as ctx:
        held = ctx.enter_context(tc.tile_pool(name="held", bufs=1))
        psum = ctx.enter_context(tc.psum_pool(name="psum", bufs=1))

        rel_list = held.tile([P, SLOTS // PER_COLUMN], U16, name="rel_list")
        irr_list = held.tile([P, SLOTS // PER_COLUMN], U16, name="irr_list")
        cand_list = held.tile([P, G // PER_COLUMN], U16, name="cand_list")
        rel_pair = held.tile([P, 2, T], F32, name="rel_pair")
        query_pair = held.tile([P, 2, Q], F32, name="query_pair", align_bytes=64)
        rel_rows = {first: rel_pair[:, 0, :], second: rel_pair[:, 1, :]}
        irr_rows = [held.tile([P, T], F32, name="irr_rows%d" % t)[:] for t in range(PACK)]
        query_rows = {first: query_pair[:, 0, :], second: query_pair[:, 1, :]}
        for t in (third, last):
            rel_rows[t] = held.tile([P, T], F32, name="rel_rows%d" % t)[:]
            query_rows[t] = held.tile([P, PACK * CUT + SLOTS if t == third else Q], F32, name="query_rows%d" % t,
                                      tag="query_slot%d" % t, align_bytes=64)[:]
        words_all = held.tile([P, U], U16, name="words_all")
        scales_all = held.tile([P, U], U8, name="scales_all")
        fa_sb = held.tile([P, PACK], F32, name="fa_sb")
        fb_sb = held.tile([P, PACK], F32, name="fb_sb")
        fa_scaled = held.tile([P, PACK], F32, name="fa_scaled")
        fb_scaled = held.tile([P, PACK], F32, name="fb_scaled")

        rel_v = rel.rearrange("(p t) c -> p t c", t=PACK)
        irr_v = irr.rearrange("(p t) c -> p t c", t=PACK)
        query_v = query.rearrange("(p t) c -> p t c", t=PACK)

        picked_scale = held.tile([P, G], U8, name="picked_scale")
        nc.vector.memset(scales_all[0:SCALE_BASE, :].bitcast(I32), 0)

        nc.sync.dma_start(cand_list[:], offs3)
        nc.scalar.dma_start(scales_all[SCALE_BASE:P, :].bitcast(I32), cand_scales[0].bitcast(I32))
        nc.sync.dma_start(rel_list[:], offs)
        nc.sync.dma_start(irr_list[:], offs2)
        nc.sync.dma_start(rel_pair[:], rel_v[:, first:second + 1, :])
        nc.scalar.dma_start(fa_sb[:], fa.rearrange("(p t) o -> p (t o)", t=PACK))
        nc.scalar.dma_start(fb_sb[:], fb.rearrange("(p t) o -> p (t o)", t=PACK))
        for t in (first, second):
            nc.sync.dma_start(irr_rows[t], irr_v[:, t, :])
        nc.sync.dma_start(query_pair[:], query_v[:, first:second + 1, :])
        for t in (third, last):
            nc.sync.dma_start(rel_rows[t], rel_v[:, t, :])
            nc.sync.dma_start(irr_rows[t], irr_v[:, t, :])
        nc.sync.dma_start(query_rows[third][:, 0:Q], query_v[:, third, :])
        nc.sync.dma_start(words_all[:].bitcast(I32), cand_words[0].bitcast(I32))
        nc.sync.dma_start(query_rows[last], query_v[:, last, :])

        nc.scalar.activation(fa_scaled[:], fa_sb[:], IDENT, scale=1.0 / (SLOTS * SLOTS))
        nc.scalar.activation(fb_scaled[:], fb_sb[:], IDENT, scale=-1.0 / SLOTS)

        cand_code = [held.tile([P, HALF], U16, name="cand_code0", align_bytes=64)]
        nc.vector.tensor_copy(picked_scale[:], scales_all[:].indirect(cand_list[:]))

        x_bf = held.tile([P, PACK, P, PACK], BF16, name="x_bf", align_bytes=64)
        x_view = x_bf[:].rearrange("p r s t -> p t s r")
        shift = {}

        def by_group(columns):
            return columns.rearrange("p (s r) -> p s r", r=PACK)

        def add_shift_scalar(t, lo, hi):
            nc.scalar.activation(x_view[:, t, :, lo:hi], by_group(query_rows[t])[:, :, lo:hi], IDENT,
                                 bias=shift[t][:])

        def add_shift_vector(t, lo, hi):
            nc.vector.tensor_scalar(x_view[:, t, :, lo:hi], by_group(query_rows[t])[:, :, lo:hi], shift[t][:],
                                    None, ADD)

        picks, shares = {}, {}
        for t in (first, second):
            picks[t] = [held.tile([P, SLOTS], F32, name="%s_pick%d" % (side, t)) for side in ("rel", "irr")]
            shares[t] = held.tile([P, 1], F32, name="rel_share%d" % t)
            shift[t] = held.tile([P, 1], F32, name="shift%d" % t)
        nc.vector.tensor_copy(picks[first][0][:], rel_rows[first].indirect(rel_list[:]))
        nc.scalar.activation(picks[second][0][:], rel_rows[second].indirect(rel_list[:]), COPY)
        for t in (first, second):
            rel_terms = held.tile([P, SLOTS], F32, name="rel_terms%d" % t)
            nc.scalar.activation(rel_terms[:], picks[t][0][:], IDENT, scale=fa_scaled[:, t:t + 1],
                                 accum_out=shares[t][:])
        for t in (first, second):
            nc.vector.tensor_copy(picks[t][1][:], irr_rows[t].indirect(irr_list[:]))
            irr_terms = held.tile([P, SLOTS], F32, name="irr_terms%d" % t)
            nc.scalar.activation(irr_terms[:], picks[t][1][:], IDENT, scale=fb_scaled[:, t:t + 1],
                                 bias=shares[t][:], accum_out=shift[t][:])
        for lo in (0, 2):
            add_shift_vector(first, lo, lo + 2)
        add_shift_scalar(second, 0, PACK)
        for t in (third, last):
            rel_pick = held.tile([P, SLOTS], F32, name="rel_pick%d" % t)
            irr_pick = held.tile([P, SLOTS], F32, name="irr_pick%d" % t)
            rel_terms = held.tile([P, SLOTS], F32, name="rel_terms%d" % t)
            rel_share = held.tile([P, 1], F32, name="rel_share%d" % t)
            shift[t] = held.tile([P, 1], F32, name="shift%d" % t)
            nc.vector.tensor_copy(rel_pick[:], rel_rows[t].indirect(rel_list[:]))
            nc.scalar.activation(rel_terms[:], rel_pick[:], IDENT, scale=fa_scaled[:, t:t + 1], accum_out=rel_share[:])
            nc.vector.tensor_copy(irr_pick[:], irr_rows[t].indirect(irr_list[:]))
            if t == last:
                low_words = by_group(query_rows[third][:, 0:PACK * CUT])
                for lo in (0, 2):
                    nc.vector.tensor_scalar(x_view[:, third, 0:CUT, lo:lo + 2], low_words[:, :, lo:lo + 2],
                                            shift[third][:], None, ADD)
                nc.scalar.activation(x_view[:, third, CUT:P, :], by_group(query_rows[third][:, PACK * CUT:Q]),
                                     IDENT, bias=shift[third][:])
                irr_terms = query_rows[third][:, PACK * CUT:PACK * CUT + SLOTS]
            else:
                irr_terms = held.tile([P, SLOTS], F32, name="irr_terms%d" % t)[:]
            nc.scalar.activation(irr_terms, irr_pick[:], IDENT, scale=fb_scaled[:, t:t + 1], bias=rel_share[:],
                                 accum_out=shift[t][:])

        cand_scale = held.tile([P, G], U8, name="cand_scale", align_bytes=64)
        nc.vector.memset(cand_scale[:].bitcast(I32), 0)
        for quad in range(4):
            rows = slice(SCALE_BASE + 4 * quad, SCALE_BASE + 4 * quad + 4)
            nc.sync.dma_start(cand_scale[32 * quad:32 * quad + 4, :].bitcast(I32), picked_scale[rows, :].bitcast(I32))
        nc.vector.tensor_copy(cand_code[0][:], words_all[:].indirect(cand_list[:, 0:HALF // PER_COLUMN]))

        for r in (3, 2):
            add_shift_scalar(last, r, r + 1)
        for r in (0, 1):
            add_shift_vector(last, r, r + 1)

        x_code = held.tile([P, Q], U32, name="x_code", align_bytes=64)
        x_scale = held.tile([P, Q], U8, name="x_scale", align_bytes=64)
        for r in (0, 1, 3, 2):
            cols = slice(r * P, (r + 1) * P)
            nc.vector.quantize_mx(out=x_code[:, cols].bitcast(FP8X4), scales=x_scale[:, cols],
                                  in_=x_bf[:, r].rearrange("p s t -> p (s t)"))
        cand_code.append(held.tile([P, HALF], U16, name="cand_code1", tag="query_slot%d" % last, align_bytes=64))
        nc.vector.tensor_copy(cand_code[1][:], words_all[:].indirect(cand_list[:, HALF // PER_COLUMN:G // PER_COLUMN]))

        y_code = held.tile([P, G], U32, name="y_code", align_bytes=64)
        y_scale = held.tile([P, G], U8, name="y_scale", align_bytes=64)
        out0_v = out_0.rearrange("(p r) g -> p r g", r=PACK)
        out1_v = out_1[0].rearrange("p c t -> p (c t)").bitcast(I32)
        out2_v = out_2[0].bitcast(I32)
        y_half = [held.tile([P, PACK, HALF], F32, name="y_half%d" % h) for h in range(2)]
        y_bf = [held.tile([P, HALF, PACK], BF16, name="y_bf%d" % h, align_bytes=64) for h in range(2)]

        def multiply(target, r, h, lo, width):
            rows = slice(r * P, (r + 1) * P)
            nc.tensor.matmul_mx(out=target, lhsT=x_code[:, rows].bitcast(FP8X4), lhsT_scale=x_scale[:, rows],
                                rhs=cand_code[h][:, lo:lo + width].bitcast(FP4X4),
                                rhs_scale=cand_scale[:, h * HALF + lo:h * HALF + lo + width], start=True, stop=True)

        def product(r, h, lo, width, bank_tag):
            bank = psum.tile([P, width], F32, name="bank%d_%d_%d" % (h, r, lo), tag=bank_tag)
            multiply(bank[:], r, h, lo, width)
            nc.scalar.copy(y_half[h][:, r, lo:lo + width], bank[:])

        def pair_product(r, h, lo, bank_tag):
            bank = psum.tile([P, 2, CHUNK], F32, name="pair%d_%d_%d" % (h, r, lo), tag=bank_tag)
            for e in range(2):
                multiply(bank[:, e, :], r + e, h, lo, CHUNK)
            nc.scalar.copy(y_half[h][:, r:r + 2, lo:lo + CHUNK], bank[:])

        def interleave(h, lo, width):
            nc.vector.tensor_copy(y_bf[h][:, lo:lo + width, :].rearrange("p (c i) r -> p c r i", i=RUN),
                                  y_half[h][:, :, lo:lo + width].rearrange("p r (c i) -> p c r i", i=RUN))

        def quantise(h, lo, width):
            cols = slice(h * HALF + lo, h * HALF + lo + width)
            nc.vector.quantize_mx(out=y_code[:, cols].bitcast(FP8X4), scales=y_scale[:, cols],
                                  in_=y_bf[h][:, lo:lo + width, :].rearrange("p g r -> p (g r)"))

        def store_rows(h, r):
            nc.sync.dma_start(out0_v[:, r:r + 2, h * HALF:(h + 1) * HALF], y_half[h][:, r:r + 2, :])

        for r in (0, 1):
            product(r, 0, 0, HALF, "bank%d" % r)
        store_rows(0, 0)
        product(3, 0, 0, CHUNK, "bank2")
        product(2, 0, 0, CHUNK, "bank3")
        interleave(0, 0, CHUNK)
        pair_product(2, 0, CHUNK, "bank4")
        interleave(0, CHUNK, CHUNK)
        store_rows(0, 2)
        for c in range(2):
            quantise(0, c * CHUNK, CHUNK)

        pair_product(0, 1, 0, "bank5")
        pair_product(2, 1, 0, "bank6")
        interleave(1, 0, CHUNK)
        pair_product(0, 1, CHUNK, "bank7")
        store_rows(1, 0)
        product(2, 1, CHUNK, CHUNK, "bank0")
        product(3, 1, CHUNK, TAIL, "bank1")
        product(3, 1, CHUNK + TAIL, TAIL, "bank2")
        store_rows(1, 2)
        interleave(1, CHUNK, TAIL)
        quantise(1, 0, CHUNK)
        interleave(1, CHUNK + TAIL, TAIL)
        quantise(1, CHUNK, TAIL)
        quantise(1, CHUNK + TAIL, TAIL)

        nc.scalar.dma_start(out1_v, y_code[:].bitcast(I32))
        for quad in range(4):
            nc.sync.dma_start(out2_v[4 * quad:4 * quad + 4, :], y_scale[32 * quad:32 * quad + 4, :].bitcast(I32))
